import numpy as np
import ml_dtypes


def mxq(x, axis, fmt="e4m3"):
    dtype, down = {"e4m3": (ml_dtypes.float8_e4m3fn, 7), "e5m2": (ml_dtypes.float8_e5m2, 14)}[fmt]
    v = np.moveaxis(np.asarray(x, np.float32).astype(ml_dtypes.bfloat16).astype(np.float64), axis, -1)
    blocks = v.reshape(v.shape[:-1] + (-1, 32))
    amax = np.abs(blocks).max(-1, keepdims=True)
    byte = np.maximum(np.where(amax > 0, np.frexp(amax)[1] - 1 + 127, 0) - down, 1)
    scale = np.exp2(byte - 127.0)
    codes = (blocks / scale).astype(np.float32).astype(dtype).astype(np.float64)
    return np.moveaxis((codes * scale).reshape(v.shape), -1, axis)


WIDE = False


def mx_kscale(k):
    if not WIDE:
        return np.ones(k)
    levels = np.array([10, -10, 5, -5, 0])
    if k % 512:
        return np.exp2(np.random.permutation(np.resize(levels, k // 32))).repeat(32)
    a = np.empty((k // 512, 16))
    for p in range(k // 512):
        a[p, :8] = np.random.permutation(np.resize(levels, 8))
        for g in range(8):
            far = levels[np.abs(levels - a[p, g]) >= 10]
            a[p, g + 8] = far[np.random.randint(len(far))]
    return np.exp2(a.ravel()).repeat(32)


def f64(x):
    return np.asarray(x).astype(np.float64)


def striped(idx):
    return np.tile(idx.reshape(-1, 16).T, (8, 1)).astype(np.uint16)


def unstriped(offs):
    return offs[:16].T.reshape(-1).astype(np.int64)


E2M1 = np.array([0.0, 0.5, 1.0, 1.5, 2.0, 3.0, 4.0, 6.0, -0.0, -0.5, -1.0, -1.5, -2.0, -3.0, -4.0, -6.0])


def pack_fp4(w):
    k, n = w.shape
    w = f64(np.asarray(w, np.float32).astype(ml_dtypes.bfloat16)).reshape(k // 32, 32, n)
    amax = np.abs(w).max(1)
    mant, ex = np.frexp(amax / 6.0)
    byte = np.clip(np.where(amax > 0, np.where(mant > 0.5, ex, ex - 1) + 127, 1), 1, 254)
    scaled = (w * np.exp2(127.0 - byte)[:, None, :]).reshape(k, n).astype(np.float32)
    c = np.ascontiguousarray(scaled.reshape(k // 512, 128, 4, n).transpose(0, 1, 3, 2)).astype(ml_dtypes.float4_e2m1fn).view(np.uint8) & 0xF
    words = (c[..., 0::2] | (c[..., 1::2] << 4)).reshape(k // 512, 128, 2 * n)
    return np.ascontiguousarray(words), np.ascontiguousarray(byte.astype(np.uint8).reshape(k // 512, 16, n))


def unpack_fp4(words, scales):
    g, _, n = scales.shape
    words = np.ascontiguousarray(words).reshape(g, 128, n, 2)
    nib = np.empty((g, 128, n, 4), np.uint8)
    nib[..., 0::2] = words & 0xF
    nib[..., 1::2] = words >> 4
    vals = E2M1[nib] * np.repeat(np.exp2(scales.astype(np.float64) - 127.0), 8, axis=1)[..., None]
    return vals.transpose(0, 1, 3, 2).reshape(g * 512, n)


K, T, S, V, N = 512, 4096, 1024, 512, 128
P = 2 ** 7


def setup_inputs():
    n = np.random.standard_normal
    s = mx_kscale(K)[:, None]
    packed_w1 = pack_fp4(n((K, N)) / np.sqrt(K) / s)
    return {
        "xT": (n((K, T)) * s).astype(np.float32),
        "w1_words": packed_w1[0],
        "w1_scales": packed_w1[1],
        "fx": np.tile(np.random.uniform(0.05, 0.95, V), (P, 1)).astype(np.float32),
        "fy": np.tile(np.random.uniform(0.05, 0.95, V), (P, 1)).astype(np.float32),
        "offs": striped(np.random.permutation(T)[:S]),
        "c00": striped(np.random.permutation(S)[:V]),
        "c01": striped(np.random.permutation(S)[:V]),
        "c10": striped(np.random.permutation(S)[:V]),
        "c11": striped(np.random.permutation(S)[:V]),
    }


def reference(xT, w1_words, w1_scales, fx, fy, offs, c00, c01, c10, c11):
    xq = mxq(f64(xT)[:, unstriped(offs)], 0, "e4m3")
    y = unpack_fp4(w1_words, w1_scales).T @ xq
    top = y[:, unstriped(c00)] + (y[:, unstriped(c01)] - y[:, unstriped(c00)]) * f64(fx)[:1]
    low = y[:, unstriped(c10)] + (y[:, unstriped(c11)] - y[:, unstriped(c10)]) * f64(fx)[:1]
    return top + (low - top) * f64(fy)[:1]

@@ -1,0 +1,104 @@
+import concourse.mybir as mybir
+from concourse.masks import make_identity
+from contextlib import ExitStack
+
+K, T, S, V, N = 512, 4096, 1024, 512, 128
+FLOPS = 2 * K * S * N
+
+F32 = mybir.dt.float32
+BF16 = mybir.dt.bfloat16
+I32 = mybir.dt.int32
+U32 = mybir.dt.uint32
+U16 = mybir.dt.uint16
+U8 = mybir.dt.uint8
+FP8X4 = mybir.dt.float8_e4m3fn_x4
+FP4X4 = mybir.dt.float4_e2m1fn_x4
+MULT = mybir.AluOpType.mult
+ADD = mybir.AluOpType.add
+COPY = mybir.ActivationFunctionType.Copy
+
+P = 128
+PACK = 4
+
+
+def tile_picked_bilin_none_e_kernel(tc, xT, w1_words, w1_scales, fx, fy, offs, c00, c01, c10, c11, out):
+    nc = tc.nc
+    with ExitStack() as ctx:
+        sb = ctx.enter_context(tc.tile_pool(name="sb", bufs=1))
+        ps = ctx.enter_context(tc.psum_pool(name="ps", bufs=1))
+
+        frows = sb.tile([P, P], F32, name="frows")
+        nc.vector.memset(frows[:], 0.0)
+        picks = sb.tile([P, S // 16], U16, name="picks")
+        rows = xT.rearrange("(p j) t -> p j t", j=PACK)
+        planes = [sb.tile([P, T], F32, name=f"plane{j}") for j in range(PACK)]
+        nc.sync.dma_start(planes[0][:], rows[:, 0, :])
+        nc.sync.dma_start(picks[:], offs)
+        nc.sync.dma_start(frows[0:4, :], fx[0, :].rearrange("(b c) -> b c", b=4))
+        nc.sync.dma_start(frows[4:8, :], fy[0, :].rearrange("(b c) -> b c", b=4))
+        for j in range(1, PACK):
+            nc.sync.dma_start(planes[j][:], rows[:, j, :])
+        corners = []
+        for i, src in enumerate((c00, c01, c10, c11)):
+            lst = sb.tile([P, V // 16], U16, name=f"corner{i}")
+            nc.sync.dma_start(lst[:], src)
+            corners.append(lst)
+
+        wscale = sb.tile([P, N], U8, name="wscale", align_bytes=64)
+        nc.gpsimd.memset(wscale[:], 0)
+        ident = sb.tile([P, P], F32, name="ident")
+        make_identity(nc, ident[:])
+        wwords = sb.tile([P, 2 * N], U8, name="wwords", align_bytes=64)
+        nc.gpsimd.dma_start(wwords[:].bitcast(I32), w1_words[0].bitcast(I32))
+        for q in range(4):
+            nc.gpsimd.dma_start(wscale[32 * q:32 * q + 4, :].bitcast(I32), w1_scales[0, 4 * q:4 * q + 4, :].bitcast(I32))
+
+        fps = ps.tile([P, P], F32, name="fps")
+        nc.tensor.transpose(fps[:], frows[:], ident[:])
+        f = sb.tile([P, 2, 8], F32, name="f")
+        nc.scalar.copy(f[:, 1, :], fps[:, 0:8])
+        nc.scalar.activation(f[:, 0, :], fps[:, 0:8], COPY, bias=1.0, scale=-1.0)
+        wcol = sb.tile([P, 4, 4], F32, name="wcol")
+        for a in range(2):
+            for b in range(2):
+                nc.gpsimd.tensor_tensor(wcol[:, 2 * a + b, :], f[:, a, 4:8], f[:, b, 0:4], MULT)
+        wts = []
+        for i in range(4):
+            wps = ps.tile([P, V], F32, name=f"wps{i}")
+            for b in range(4):
+                nc.tensor.transpose(wps[:, b * P:(b + 1) * P], wcol[:, i, b:b + 1].to_broadcast([P, P]), ident[:])
+            wt = sb.tile([P, V], F32, name=f"wt{i}")
+            nc.scalar.copy(wt[:], wps[:])
+            wts.append(wt)
+
+        halves = [sb.tile([P, 512, PACK], BF16, name=f"xb{h}", align_bytes=64) for h in range(2)]
+        for j in range(PACK):
+            for h in range(2):
+                nc.vector.tensor_copy(halves[h][:, :, j], planes[j][:].indirect(picks[:, 32 * h:32 * h + 32]))
+        y = sb.tile([P, S], F32, name="y")
+        chunks = [(0, 0, 512), (1, 0, 256), (1, 256, 256)]
+        for ci, (h, c0, n) in enumerate(chunks):
+            codes = sb.tile([P, n], U32, name=f"codes{ci}", align_bytes=64)
+            scales = sb.tile([P, n], U8, name=f"scales{ci}", align_bytes=64)
+            nc.vector.quantize_mx(out=codes[:].bitcast(FP8X4), scales=scales[:], in_=halves[h][:, c0:c0 + n, :].rearrange("p n j -> p (n j)"))
+            acc = ps.tile([P, n], F32, name=f"acc{ci}")
+            nc.tensor.matmul_mx(out=acc[:], lhsT=wwords[:].bitcast(FP4X4), lhsT_scale=wscale[:], rhs=codes[:].bitcast(FP8X4), rhs_scale=scales[:], start=True, stop=True)
+            dst = y[:, 512 * h + c0:512 * h + c0 + n]
+            if ci == len(chunks) - 1:
+                nc.vector.tensor_copy(dst, acc[:])
+            else:
+                nc.scalar.copy(dst, acc[:])
+
+        terms = [sb.tile([P, V], F32, name=f"term{i}") for i in range(4)]
+        s01 = sb.tile([P, V], F32, name="s01")
+        s012 = sb.tile([P, V], F32, name="s012")
+        for i in range(3):
+            nc.vector.tensor_tensor(terms[i][:], y[:].indirect(corners[i][:]), wts[i][:], MULT)
+        nc.vector.tensor_tensor(s01[:], terms[0][:], terms[1][:], ADD)
+        nc.vector.tensor_tensor(terms[3][:], y[:].indirect(corners[3][:]), wts[3][:], MULT)
+        nc.vector.tensor_tensor(s012[:], s01[:], terms[2][:], ADD)
+        for h in range(2):
+            cols = slice(256 * h, 256 * h + 256)
+            res = sb.tile([P, 256], F32, name=f"res{h}")
+            nc.vector.tensor_tensor(res[:], s012[:, cols], terms[3][:, cols], ADD)
+            (nc.sync if h == 0 else nc.scalar).dma_start(out[:, cols], res[:])

@@ -36,8 +36,11 @@ def tile_picked_bilin_none_e_kernel(tc, xT, w1_words, w1_scales, fx, fy, offs, c
         nc.sync.dma_start(picks[:], offs)
         nc.sync.dma_start(frows[0:4, :], fx[0, :].rearrange("(b c) -> b c", b=4))
         nc.sync.dma_start(frows[4:8, :], fy[0, :].rearrange("(b c) -> b c", b=4))
-        for j in range(1, PACK):
+        for j in range(1, PACK - 1):
             nc.sync.dma_start(planes[j][:], rows[:, j, :])
+        pieces = [(0, 2048), (2048, 3072), (3072, 3584), (3584, 4096)]
+        for a, b in pieces:
+            nc.sync.dma_start(planes[3][:, a:b], rows[:, 3, a:b])
         corners = []
         for i, src in enumerate((c00, c01, c10, c11)):
             lst = sb.tile([P, V // 16], U16, name=f"corner{i}")
@@ -53,7 +56,7 @@ def tile_picked_bilin_none_e_kernel(tc, xT, w1_words, w1_scales, fx, fy, offs, c
         for q in range(4):
             nc.gpsimd.dma_start(wscale[32 * q:32 * q + 4, :].bitcast(I32), w1_scales[0, 4 * q:4 * q + 4, :].bitcast(I32))
 
-        fps = ps.tile([P, P], F32, name="fps")
+        fps = ps.tile([P, P], F32, name="fps", tag="bank7")
         nc.tensor.transpose(fps[:], frows[:], ident[:])
         f = sb.tile([P, 2, 8], F32, name="f")
         nc.scalar.copy(f[:, 1, :], fps[:, 0:8])
@@ -64,7 +67,7 @@ def tile_picked_bilin_none_e_kernel(tc, xT, w1_words, w1_scales, fx, fy, offs, c
                 nc.gpsimd.tensor_tensor(wcol[:, 2 * a + b, :], f[:, a, 4:8], f[:, b, 0:4], MULT)
         wts = []
         for i in range(4):
-            wps = ps.tile([P, V], F32, name=f"wps{i}")
+            wps = ps.tile([P, V], F32, name=f"wps{i}", tag=f"bank{i + 3}")
             for b in range(4):
                 nc.tensor.transpose(wps[:, b * P:(b + 1) * P], wcol[:, i, b:b + 1].to_broadcast([P, P]), ident[:])
             wt = sb.tile([P, V], F32, name=f"wt{i}")
@@ -72,16 +75,24 @@ def tile_picked_bilin_none_e_kernel(tc, xT, w1_words, w1_scales, fx, fy, offs, c
             wts.append(wt)
 
         halves = [sb.tile([P, 512, PACK], BF16, name=f"xb{h}", align_bytes=64) for h in range(2)]
-        for j in range(PACK):
+        for j in range(PACK - 1):
             for h in range(2):
                 nc.vector.tensor_copy(halves[h][:, :, j], planes[j][:].indirect(picks[:, 32 * h:32 * h + 32]))
+        last = sb.tile([P, T], BF16, name="last")
+        for i, (a, b) in enumerate(pieces):
+            if i == 0:
+                nc.scalar.copy(last[:, a:b], planes[3][:, a:b])
+            else:
+                nc.vector.tensor_copy(last[:, a:b], planes[3][:, a:b])
+        nc.vector.tensor_copy(halves[0][:, :, 3], planes[3][:].indirect(picks[:, 0:32]))
+        nc.scalar.activation(halves[1][:, :, 3], last[:].indirect(picks[:, 32:64]), COPY)
         y = sb.tile([P, S], F32, name="y")
-        chunks = [(0, 0, 512), (1, 0, 256), (1, 256, 256)]
+        chunks = [(0, 0, 512), (1, 0, 256), (1, 256, 128), (1, 384, 128)]
         for ci, (h, c0, n) in enumerate(chunks):
             codes = sb.tile([P, n], U32, name=f"codes{ci}", align_bytes=64)
             scales = sb.tile([P, n], U8, name=f"scales{ci}", align_bytes=64)
             nc.vector.quantize_mx(out=codes[:].bitcast(FP8X4), scales=scales[:], in_=halves[h][:, c0:c0 + n, :].rearrange("p n j -> p (n j)"))
-            acc = ps.tile([P, n], F32, name=f"acc{ci}")
+            acc = ps.tile([P, n], F32, name=f"acc{ci}", tag=f"bank{ci}")
             nc.tensor.matmul_mx(out=acc[:], lhsT=wwords[:].bitcast(FP4X4), lhsT_scale=wscale[:], rhs=codes[:].bitcast(FP8X4), rhs_scale=scales[:], start=True, stop=True)
             dst = y[:, 512 * h + c0:512 * h + c0 + n]
             if ci == len(chunks) - 1:
@@ -89,16 +100,30 @@ def tile_picked_bilin_none_e_kernel(tc, xT, w1_words, w1_scales, fx, fy, offs, c
             else:
                 nc.scalar.copy(dst, acc[:])
 
-        terms = [sb.tile([P, V], F32, name=f"term{i}") for i in range(4)]
-        s01 = sb.tile([P, V], F32, name="s01")
-        s012 = sb.tile([P, V], F32, name="s012")
-        for i in range(3):
-            nc.vector.tensor_tensor(terms[i][:], y[:].indirect(corners[i][:]), wts[i][:], MULT)
-        nc.vector.tensor_tensor(s01[:], terms[0][:], terms[1][:], ADD)
-        nc.vector.tensor_tensor(terms[3][:], y[:].indirect(corners[3][:]), wts[3][:], MULT)
-        nc.vector.tensor_tensor(s012[:], s01[:], terms[2][:], ADD)
-        for h in range(2):
-            cols = slice(256 * h, 256 * h + 256)
-            res = sb.tile([P, 256], F32, name=f"res{h}")
-            nc.vector.tensor_tensor(res[:], s012[:, cols], terms[3][:, cols], ADD)
-            (nc.sync if h == 0 else nc.scalar).dma_start(out[:, cols], res[:])
+        groups = [(0, 256), (256, 384), (384, 512)]
+        for gi, (a, b) in enumerate(groups):
+            n = b - a
+            terms = [sb.tile([P, n], F32, name=f"term{gi}_{i}") for i in range(4)]
+            res = sb.tile([P, n], F32, name=f"res{gi}")
+            if gi < 2:
+                sums = [ps.tile([P, P], F32, name=f"sum{a // P + k}", tag=f"bank{4 + a // P + k}") for k in range(n // P)]
+                for i in range(4):
+                    nc.vector.tensor_tensor(terms[i][:], y[:].indirect(corners[i][:, a // 16:b // 16]), wts[i][:, a:b], MULT)
+                    for k in range(n // P):
+                        nc.tensor.matmul(sums[k][:], terms[i][:, k * P:(k + 1) * P], ident[:], start=(i == 0), stop=(i == 3), is_transpose=True)
+                back = ps.tile([P, n], F32, name=f"back{gi}", tag=f"bank{gi}")
+                for k in range(n // P):
+                    turned = sb.tile([P, P], F32, name=f"turned{a // P + k}")
+                    nc.scalar.copy(turned[:], sums[k][:])
+                    nc.tensor.transpose(back[:, k * P:(k + 1) * P], turned[:], ident[:])
+                nc.scalar.copy(res[:], back[:])
+            else:
+                s01 = sb.tile([P, n], F32, name="s01")
+                s012 = sb.tile([P, n], F32, name="s012")
+                for i in range(3):
+                    nc.vector.tensor_tensor(terms[i][:], y[:].indirect(corners[i][:, a // 16:b // 16]), wts[i][:, a:b], MULT)
+                nc.vector.tensor_tensor(s01[:], terms[0][:], terms[1][:], ADD)
+                nc.vector.tensor_tensor(terms[3][:], y[:].indirect(corners[3][:, a // 16:b // 16]), wts[3][:, a:b], MULT)
+                nc.vector.tensor_tensor(s012[:], s01[:], terms[2][:], ADD)
+                nc.vector.tensor_tensor(res[:], s012[:], terms[3][:], ADD)
+            nc.sync.dma_start(out[:, a:b], res[:])

@@ -38,23 +38,23 @@ def tile_picked_bilin_none_e_kernel(tc, xT, w1_words, w1_scales, fx, fy, offs, c
         nc.sync.dma_start(frows[4:8, :], fy[0, :].rearrange("(b c) -> b c", b=4))
         for j in range(1, PACK - 1):
             nc.sync.dma_start(planes[j][:], rows[:, j, :])
-        pieces = [(0, 2048), (2048, 3072), (3072, 3584), (3584, 4096)]
+        pieces = [(0, 1792), (1792, 3072), (3072, 3840), (3840, 4096)]
         for a, b in pieces:
             nc.sync.dma_start(planes[3][:, a:b], rows[:, 3, a:b])
+        wscale = sb.tile([P, N], U8, name="wscale", align_bytes=64)
+        nc.gpsimd.memset(wscale[:], 0)
+        wwords = sb.tile([P, 2 * N], U8, name="wwords", align_bytes=64)
+        nc.sync.dma_start(wwords[:].bitcast(I32), w1_words[0].bitcast(I32))
+        for q in range(4):
+            nc.sync.dma_start(wscale[32 * q:32 * q + 4, :].bitcast(I32), w1_scales[0, 4 * q:4 * q + 4, :].bitcast(I32))
         corners = []
         for i, src in enumerate((c00, c01, c10, c11)):
             lst = sb.tile([P, V // 16], U16, name=f"corner{i}")
             nc.sync.dma_start(lst[:], src)
             corners.append(lst)
 
-        wscale = sb.tile([P, N], U8, name="wscale", align_bytes=64)
-        nc.gpsimd.memset(wscale[:], 0)
         ident = sb.tile([P, P], F32, name="ident")
         make_identity(nc, ident[:])
-        wwords = sb.tile([P, 2 * N], U8, name="wwords", align_bytes=64)
-        nc.gpsimd.dma_start(wwords[:].bitcast(I32), w1_words[0].bitcast(I32))
-        for q in range(4):
-            nc.gpsimd.dma_start(wscale[32 * q:32 * q + 4, :].bitcast(I32), w1_scales[0, 4 * q:4 * q + 4, :].bitcast(I32))
 
         fps = ps.tile([P, P], F32, name="fps", tag="bank7")
         nc.tensor.transpose(fps[:], frows[:], ident[:])
@@ -79,15 +79,14 @@ def tile_picked_bilin_none_e_kernel(tc, xT, w1_words, w1_scales, fx, fy, offs, c
             for h in range(2):
                 nc.vector.tensor_copy(halves[h][:, :, j], planes[j][:].indirect(picks[:, 32 * h:32 * h + 32]))
         last = sb.tile([P, T], BF16, name="last")
-        for i, (a, b) in enumerate(pieces):
-            if i == 0:
-                nc.scalar.copy(last[:, a:b], planes[3][:, a:b])
-            else:
-                nc.vector.tensor_copy(last[:, a:b], planes[3][:, a:b])
+        for a, b in ((0, 1792), (3584, 3840), (3840, 4096)):
+            nc.scalar.copy(last[:, a:b], planes[3][:, a:b])
+        for a, b in ((1792, 3072), (3072, 3584)):
+            nc.vector.tensor_copy(last[:, a:b], planes[3][:, a:b])
         nc.vector.tensor_copy(halves[0][:, :, 3], planes[3][:].indirect(picks[:, 0:32]))
         nc.scalar.activation(halves[1][:, :, 3], last[:].indirect(picks[:, 32:64]), COPY)
         y = sb.tile([P, S], F32, name="y")
-        chunks = [(0, 0, 512), (1, 0, 256), (1, 256, 128), (1, 384, 128)]
+        chunks = [(0, 0, 256), (0, 256, 256), (1, 0, 256), (1, 256, 128), (1, 384, 128)]
         for ci, (h, c0, n) in enumerate(chunks):
             codes = sb.tile([P, n], U32, name=f"codes{ci}", align_bytes=64)
             scales = sb.tile([P, n], U8, name=f"scales{ci}", align_bytes=64)
@@ -95,7 +94,7 @@ def tile_picked_bilin_none_e_kernel(tc, xT, w1_words, w1_scales, fx, fy, offs, c
             acc = ps.tile([P, n], F32, name=f"acc{ci}", tag=f"bank{ci}")
             nc.tensor.matmul_mx(out=acc[:], lhsT=wwords[:].bitcast(FP4X4), lhsT_scale=wscale[:], rhs=codes[:].bitcast(FP8X4), rhs_scale=scales[:], start=True, stop=True)
             dst = y[:, 512 * h + c0:512 * h + c0 + n]
-            if ci == len(chunks) - 1:
+            if n == 128:
                 nc.vector.tensor_copy(dst, acc[:])
             else:
                 nc.scalar.copy(dst, acc[:])
@@ -106,7 +105,7 @@ def tile_picked_bilin_none_e_kernel(tc, xT, w1_words, w1_scales, fx, fy, offs, c
             terms = [sb.tile([P, n], F32, name=f"term{gi}_{i}") for i in range(4)]
             res = sb.tile([P, n], F32, name=f"res{gi}")
             if gi < 2:
-                sums = [ps.tile([P, P], F32, name=f"sum{a // P + k}", tag=f"bank{4 + a // P + k}") for k in range(n // P)]
+                sums = [ps.tile([P, P], F32, name=f"sum{a // P + k}", tag=f"bank{5 + a // P + k}") for k in range(n // P)]
                 for i in range(4):
                     nc.vector.tensor_tensor(terms[i][:], y[:].indirect(corners[i][:, a // 16:b // 16]), wts[i][:, a:b], MULT)
                     for k in range(n // P):
@@ -124,6 +123,8 @@ def tile_picked_bilin_none_e_kernel(tc, xT, w1_words, w1_scales, fx, fy, offs, c
                     nc.vector.tensor_tensor(terms[i][:], y[:].indirect(corners[i][:, a // 16:b // 16]), wts[i][:, a:b], MULT)
                 nc.vector.tensor_tensor(s01[:], terms[0][:], terms[1][:], ADD)
                 nc.vector.tensor_tensor(terms[3][:], y[:].indirect(corners[3][:, a // 16:b // 16]), wts[3][:, a:b], MULT)
-                nc.vector.tensor_tensor(s012[:], s01[:], terms[2][:], ADD)
-                nc.vector.tensor_tensor(res[:], s012[:], terms[3][:], ADD)
-            nc.sync.dma_start(out[:, a:b], res[:])
+                for lo in (0, 64):
+                    nc.vector.tensor_tensor(s012[:, lo:lo + 64], s01[:, lo:lo + 64], terms[2][:, lo:lo + 64], ADD)
+                for lo in (0, 64):
+                    nc.vector.tensor_tensor(res[:, lo:lo + 64], s012[:, lo:lo + 64], terms[3][:, lo:lo + 64], ADD)
+            (nc.scalar if gi == 1 else nc.sync).dma_start(out[:, a:b], res[:])

@@ -94,7 +94,7 @@ def tile_picked_bilin_none_e_kernel(tc, xT, w1_words, w1_scales, fx, fy, offs, c
             acc = ps.tile([P, n], F32, name=f"acc{ci}", tag=f"bank{ci}")
             nc.tensor.matmul_mx(out=acc[:], lhsT=wwords[:].bitcast(FP4X4), lhsT_scale=wscale[:], rhs=codes[:].bitcast(FP8X4), rhs_scale=scales[:], start=True, stop=True)
             dst = y[:, 512 * h + c0:512 * h + c0 + n]
-            if n == 128:
+            if ci == 2:
                 nc.vector.tensor_copy(dst, acc[:])
             else:
                 nc.scalar.copy(dst, acc[:])

@@ -28,14 +28,15 @@ def tile_picked_bilin_none_e_kernel(tc, xT, w1_words, w1_scales, fx, fy, offs, c
         ps = ctx.enter_context(tc.psum_pool(name="ps", bufs=1))
 
         frows = sb.tile([P, P], F32, name="frows")
-        nc.vector.memset(frows[:], 0.0)
+        nc.scalar.dma_start(frows[24:28, :], fx[0, :].rearrange("(b c) -> b c", b=4))
+        nc.scalar.dma_start(frows[28:32, :], fy[0, :].rearrange("(b c) -> b c", b=4))
+        for lo, hi in ((0, 24), (32, 64), (64, 128)):
+            nc.vector.memset(frows[lo:hi, :], 0.0)
         picks = sb.tile([P, S // 16], U16, name="picks")
         rows = xT.rearrange("(p j) t -> p j t", j=PACK)
         planes = [sb.tile([P, T], F32, name=f"plane{j}") for j in range(PACK)]
         nc.sync.dma_start(planes[0][:], rows[:, 0, :])
         nc.sync.dma_start(picks[:], offs)
-        nc.sync.dma_start(frows[0:4, :], fx[0, :].rearrange("(b c) -> b c", b=4))
-        nc.sync.dma_start(frows[4:8, :], fy[0, :].rearrange("(b c) -> b c", b=4))
         for j in range(1, PACK - 1):
             nc.sync.dma_start(planes[j][:], rows[:, j, :])
         pieces = [(0, 1792), (1792, 3072), (3072, 3840), (3840, 4096)]
@@ -59,8 +60,8 @@ def tile_picked_bilin_none_e_kernel(tc, xT, w1_words, w1_scales, fx, fy, offs, c
         fps = ps.tile([P, P], F32, name="fps", tag="bank7")
         nc.tensor.transpose(fps[:], frows[:], ident[:])
         f = sb.tile([P, 2, 8], F32, name="f")
-        nc.scalar.copy(f[:, 1, :], fps[:, 0:8])
-        nc.scalar.activation(f[:, 0, :], fps[:, 0:8], COPY, bias=1.0, scale=-1.0)
+        nc.scalar.copy(f[:, 1, :], fps[:, 24:32])
+        nc.scalar.activation(f[:, 0, :], fps[:, 24:32], COPY, bias=1.0, scale=-1.0)
         wcol = sb.tile([P, 4, 4], F32, name="wcol")
         for a in range(2):
             for b in range(2):
@@ -99,32 +100,40 @@ def tile_picked_bilin_none_e_kernel(tc, xT, w1_words, w1_scales, fx, fy, offs, c
             else:
                 nc.scalar.copy(dst, acc[:])
 
-        groups = [(0, 256), (256, 384), (384, 512)]
-        for gi, (a, b) in enumerate(groups):
-            n = b - a
-            terms = [sb.tile([P, n], F32, name=f"term{gi}_{i}") for i in range(4)]
-            res = sb.tile([P, n], F32, name=f"res{gi}")
-            if gi < 2:
-                sums = [ps.tile([P, P], F32, name=f"sum{a // P + k}", tag=f"bank{5 + a // P + k}") for k in range(n // P)]
-                for i in range(4):
-                    nc.vector.tensor_tensor(terms[i][:], y[:].indirect(corners[i][:, a // 16:b // 16]), wts[i][:, a:b], MULT)
-                    for k in range(n // P):
-                        nc.tensor.matmul(sums[k][:], terms[i][:, k * P:(k + 1) * P], ident[:], start=(i == 0), stop=(i == 3), is_transpose=True)
-                back = ps.tile([P, n], F32, name=f"back{gi}", tag=f"bank{gi}")
-                for k in range(n // P):
-                    turned = sb.tile([P, P], F32, name=f"turned{a // P + k}")
-                    nc.scalar.copy(turned[:], sums[k][:])
-                    nc.tensor.transpose(back[:, k * P:(k + 1) * P], turned[:], ident[:])
-                nc.scalar.copy(res[:], back[:])
-            else:
-                s01 = sb.tile([P, n], F32, name="s01")
-                s012 = sb.tile([P, n], F32, name="s012")
-                for i in range(3):
-                    nc.vector.tensor_tensor(terms[i][:], y[:].indirect(corners[i][:, a // 16:b // 16]), wts[i][:, a:b], MULT)
-                nc.vector.tensor_tensor(s01[:], terms[0][:], terms[1][:], ADD)
-                nc.vector.tensor_tensor(terms[3][:], y[:].indirect(corners[3][:, a // 16:b // 16]), wts[3][:, a:b], MULT)
-                for lo in (0, 64):
-                    nc.vector.tensor_tensor(s012[:, lo:lo + 64], s01[:, lo:lo + 64], terms[2][:, lo:lo + 64], ADD)
-                for lo in (0, 64):
-                    nc.vector.tensor_tensor(res[:, lo:lo + 64], s012[:, lo:lo + 64], terms[3][:, lo:lo + 64], ADD)
-            (nc.scalar if gi == 1 else nc.sync).dma_start(out[:, a:b], res[:])
+        terms = [sb.tile([P, V], F32, name=f"term{i}") for i in range(4)]
+        sums = [ps.tile([P, P], F32, name=f"sum{k}", tag=f"bank{5 + k}") for k in range(3)]
+
+        def weigh(i, a, b):
+            nc.vector.tensor_tensor(terms[i][:, a:b], y[:].indirect(corners[i][:, a // 16:b // 16]), wts[i][:, a:b], MULT)
+            for k in range(a // P, min(b // P, 3)):
+                nc.tensor.matmul(sums[k][:], terms[i][:, k * P:(k + 1) * P], ident[:], start=(i == 0), stop=(i == 3), is_transpose=True)
+
+        def finish(k, queue):
+            turned = sb.tile([P, P], F32, name=f"turned{k}")
+            nc.scalar.copy(turned[:], sums[k][:])
+            back = ps.tile([P, P], F32, name=f"back{k}", tag=f"bank{k}")
+            nc.tensor.transpose(back[:], turned[:], ident[:])
+            res = sb.tile([P, P], F32, name=f"res{k}")
+            nc.scalar.copy(res[:], back[:])
+            queue.dma_start(out[:, k * P:(k + 1) * P], res[:])
+
+        for i in range(2):
+            weigh(i, 0, 3 * P)
+        for k in range(3):
+            for i in range(2, 4):
+                weigh(i, k * P, (k + 1) * P)
+            finish(k, nc.scalar if k == 2 else nc.sync)
+
+        a = 3 * P
+        s01 = sb.tile([P, P], F32, name="s01")
+        s012 = sb.tile([P, P], F32, name="s012")
+        res = sb.tile([P, P], F32, name="res3")
+        for i in range(3):
+            weigh(i, a, V)
+        nc.vector.tensor_tensor(s01[:], terms[0][:, a:V], terms[1][:, a:V], ADD)
+        weigh(3, a, V)
+        for lo in (0, 64):
+            nc.vector.tensor_tensor(s012[:, lo:lo + 64], s01[:, lo:lo + 64], terms[2][:, a + lo:a + lo + 64], ADD)
+        for lo in (0, 64):
+            nc.vector.tensor_tensor(res[:, lo:lo + 64], s012[:, lo:lo + 64], terms[3][:, a + lo:a + lo + 64], ADD)
+        nc.sync.dma_start(out[:, a:V], res[:])

@@ -39,7 +39,7 @@ def tile_picked_bilin_none_e_kernel(tc, xT, w1_words, w1_scales, fx, fy, offs, c
         nc.sync.dma_start(picks[:], offs)
         for j in range(1, PACK - 1):
             nc.sync.dma_start(planes[j][:], rows[:, j, :])
-        pieces = [(0, 1792), (1792, 3072), (3072, 3840), (3840, 4096)]
+        pieces = ((0, 1792), (1792, 3072), (3072, 3840), (3840, 4096))
         for a, b in pieces:
             nc.sync.dma_start(planes[3][:, a:b], rows[:, 3, a:b])
         wscale = sb.tile([P, N], U8, name="wscale", align_bytes=64)
@@ -87,7 +87,7 @@ def tile_picked_bilin_none_e_kernel(tc, xT, w1_words, w1_scales, fx, fy, offs, c
         nc.vector.tensor_copy(halves[0][:, :, 3], planes[3][:].indirect(picks[:, 0:32]))
         nc.scalar.activation(halves[1][:, :, 3], last[:].indirect(picks[:, 32:64]), COPY)
         y = sb.tile([P, S], F32, name="y")
-        chunks = [(0, 0, 256), (0, 256, 256), (1, 0, 256), (1, 256, 128), (1, 384, 128)]
+        chunks = ((0, 0, 256), (0, 256, 256), (1, 0, 256), (1, 256, 128), (1, 384, 128))
         for ci, (h, c0, n) in enumerate(chunks):
             codes = sb.tile([P, n], U32, name=f"codes{ci}", align_bytes=64)
             scales = sb.tile([P, n], U8, name=f"scales{ci}", align_bytes=64)
@@ -95,45 +95,49 @@ def tile_picked_bilin_none_e_kernel(tc, xT, w1_words, w1_scales, fx, fy, offs, c
             acc = ps.tile([P, n], F32, name=f"acc{ci}", tag=f"bank{ci}")
             nc.tensor.matmul_mx(out=acc[:], lhsT=wwords[:].bitcast(FP4X4), lhsT_scale=wscale[:], rhs=codes[:].bitcast(FP8X4), rhs_scale=scales[:], start=True, stop=True)
             dst = y[:, 512 * h + c0:512 * h + c0 + n]
-            if ci == 2:
+            if ci in (2, ):
                 nc.vector.tensor_copy(dst, acc[:])
             else:
                 nc.scalar.copy(dst, acc[:])
 
-        terms = [sb.tile([P, V], F32, name=f"term{i}") for i in range(4)]
-        sums = [ps.tile([P, P], F32, name=f"sum{k}", tag=f"bank{5 + k}") for k in range(3)]
+        terms = [sb.tile([P, V], F32, name=f"term{i}") for i in range(3)]
+        sums = [ps.tile([P, P], F32, name=f"sum{k}", tag=f"bank{4 + k}") for k in range(4)]
 
-        def weigh(i, a, b):
-            nc.vector.tensor_tensor(terms[i][:, a:b], y[:].indirect(corners[i][:, a // 16:b // 16]), wts[i][:, a:b], MULT)
-            for k in range(a // P, min(b // P, 3)):
-                nc.tensor.matmul(sums[k][:], terms[i][:, k * P:(k + 1) * P], ident[:], start=(i == 0), stop=(i == 3), is_transpose=True)
+        def weigh(dst, i, a, b):
+            nc.vector.tensor_tensor(dst, y[:].indirect(corners[i][:, a // 16:b // 16]), wts[i][:, a:b], MULT)
 
-        def finish(k, queue):
+        def add_up(i, k):
+            nc.tensor.matmul(sums[k][:], terms[i][:, k * P:(k + 1) * P], ident[:], start=(i == 0), stop=(i == 2), is_transpose=True)
+
+        for i in range(2):
+            weigh(terms[i][:], i, 0, V)
+            for k in range(4):
+                add_up(i, k)
+        backs = []
+        for k in range(4):
+            weigh(terms[2][:, k * P:(k + 1) * P], 2, k * P, (k + 1) * P)
+            add_up(2, k)
             turned = sb.tile([P, P], F32, name=f"turned{k}")
             nc.scalar.copy(turned[:], sums[k][:])
             back = ps.tile([P, P], F32, name=f"back{k}", tag=f"bank{k}")
             nc.tensor.transpose(back[:], turned[:], ident[:])
+            backs.append(back)
+        fourth = []
+
+        def gather_fourth(k):
+            t = sb.tile([P, P], F32, name=f"fourth{k}", tag="fourth", bufs=3)
+            weigh(t[:], 3, k * P, (k + 1) * P)
+            fourth.append(t)
+
+        def finish(k):
             res = sb.tile([P, P], F32, name=f"res{k}")
-            nc.scalar.copy(res[:], back[:])
-            queue.dma_start(out[:, k * P:(k + 1) * P], res[:])
+            nc.vector.tensor_tensor(res[:], fourth[k][:], backs[k][:], ADD)
+            nc.sync.dma_start(out[:, k * P:(k + 1) * P], res[:])
 
-        for i in range(2):
-            weigh(i, 0, 3 * P)
         for k in range(3):
-            for i in range(2, 4):
-                weigh(i, k * P, (k + 1) * P)
-            finish(k, nc.scalar if k == 2 else nc.sync)
-
-        a = 3 * P
-        s01 = sb.tile([P, P], F32, name="s01")
-        s012 = sb.tile([P, P], F32, name="s012")
-        res = sb.tile([P, P], F32, name="res3")
-        for i in range(3):
-            weigh(i, a, V)
-        nc.vector.tensor_tensor(s01[:], terms[0][:, a:V], terms[1][:, a:V], ADD)
-        weigh(3, a, V)
-        for lo in (0, 64):
-            nc.vector.tensor_tensor(s012[:, lo:lo + 64], s01[:, lo:lo + 64], terms[2][:, a + lo:a + lo + 64], ADD)
-        for lo in (0, 64):
-            nc.vector.tensor_tensor(res[:, lo:lo + 64], s012[:, lo:lo + 64], terms[3][:, a + lo:a + lo + 64], ADD)
-        nc.sync.dma_start(out[:, a:V], res[:])
+            gather_fourth(k)
+        finish(0)
+        finish(1)
+        gather_fourth(3)
+        finish(2)
+        finish(3)

@@ -117,7 +117,7 @@ def tile_picked_bilin_none_e_kernel(tc, xT, w1_words, w1_scales, fx, fy, offs, c
         for k in range(4):
             weigh(terms[2][:, k * P:(k + 1) * P], 2, k * P, (k + 1) * P)
             add_up(2, k)
-            turned = sb.tile([P, P], F32, name=f"turned{k}")
+            turned = sb.tile([P, P], F32, name=f"turned{k}", tag=f"turned{k}")
             nc.scalar.copy(turned[:], sums[k][:])
             back = ps.tile([P, P], F32, name=f"back{k}", tag=f"bank{k}")
             nc.tensor.transpose(back[:], turned[:], ident[:])
@@ -125,7 +125,7 @@ def tile_picked_bilin_none_e_kernel(tc, xT, w1_words, w1_scales, fx, fy, offs, c
         fourth = []
 
         def gather_fourth(k):
-            t = sb.tile([P, P], F32, name=f"fourth{k}", tag="fourth", bufs=3)
+            t = sb.tile([P, P], F32, name=f"fourth{k}", tag="turned0" if k == 3 else f"fourth{k}")
             weigh(t[:], 3, k * P, (k + 1) * P)
             fourth.append(t)
 

@@ -113,31 +113,28 @@ def tile_picked_bilin_none_e_kernel(tc, xT, w1_words, w1_scales, fx, fy, offs, c
             weigh(terms[i][:], i, 0, V)
             for k in range(4):
                 add_up(i, k)
-        backs = []
-        for k in range(4):
-            weigh(terms[2][:, k * P:(k + 1) * P], 2, k * P, (k + 1) * P)
-            add_up(2, k)
-            turned = sb.tile([P, P], F32, name=f"turned{k}", tag=f"turned{k}")
-            nc.scalar.copy(turned[:], sums[k][:])
-            back = ps.tile([P, P], F32, name=f"back{k}", tag=f"bank{k}")
-            nc.tensor.transpose(back[:], turned[:], ident[:])
-            backs.append(back)
-        fourth = []
+        back01 = ps.tile([P, 2 * P], F32, name="back01", tag="bank0")
+        back2 = ps.tile([P, P], F32, name="back2", tag="bank1")
+        back3 = ps.tile([P, P], F32, name="back3", tag="bank2")
+        backs = (back01[:, 0:P], back01[:, P:2 * P], back2[:], back3[:])
+        for k0, k1 in ((0, 2), (2, 3), (3, 4)):
+            weigh(terms[2][:, k0 * P:k1 * P], 2, k0 * P, k1 * P)
+            for k in range(k0, k1):
+                add_up(2, k)
+                turned = sb.tile([P, P], F32, name=f"turned{k}", tag=f"turned{k}")
+                nc.scalar.copy(turned[:], sums[k][:])
+                nc.tensor.transpose(backs[k], turned[:], ident[:])
 
-        def gather_fourth(k):
-            t = sb.tile([P, P], F32, name=f"fourth{k}", tag="turned0" if k == 3 else f"fourth{k}")
-            weigh(t[:], 3, k * P, (k + 1) * P)
-            fourth.append(t)
-
-        def finish(k):
-            res = sb.tile([P, P], F32, name=f"res{k}")
-            nc.vector.tensor_tensor(res[:], fourth[k][:], backs[k][:], ADD)
-            nc.sync.dma_start(out[:, k * P:(k + 1) * P], res[:])
-
-        for k in range(3):
-            gather_fourth(k)
-        finish(0)
-        finish(1)
-        gather_fourth(3)
-        finish(2)
-        finish(3)
+        res = sb.tile([P, V], F32, name="res")
+        first = sb.tile([P, 448], F32, name="fourth_first")
+        weigh(first[:, 0:256], 3, 0, 256)
+        weigh(first[:, 256:448], 3, 256, 448)
+        nc.vector.tensor_tensor(res[:, 0:256], first[:, 0:256], back01[:], ADD)
+        nc.sync.dma_start(out[:, 0:256], res[:, 0:256])
+        rest = sb.tile([P, 64], F32, name="fourth_rest", tag="turned1")
+        weigh(rest[:], 3, 448, V)
+        nc.vector.tensor_tensor(res[:, 256:384], first[:, 256:384], back2[:], ADD)
+        nc.sync.dma_start(out[:, 256:384], res[:, 256:384])
+        nc.vector.tensor_tensor(res[:, 384:448], first[:, 384:448], back3[:, 0:64], ADD)
+        nc.vector.tensor_tensor(res[:, 448:V], rest[:], back3[:, 64:P], ADD)
+        nc.sync.dma_start(out[:, 384:V], res[:, 384:V])

@@ -39,7 +39,7 @@ def tile_picked_bilin_none_e_kernel(tc, xT, w1_words, w1_scales, fx, fy, offs, c
         nc.sync.dma_start(picks[:], offs)
         for j in range(1, PACK - 1):
             nc.sync.dma_start(planes[j][:], rows[:, j, :])
-        pieces = ((0, 1792), (1792, 3072), (3072, 3840), (3840, 4096))
+        pieces = ((0, 1792), (1792, 3200), (3200, 3840), (3840, 4096))
         for a, b in pieces:
             nc.sync.dma_start(planes[3][:, a:b], rows[:, 3, a:b])
         wscale = sb.tile([P, N], U8, name="wscale", align_bytes=64)
@@ -80,9 +80,9 @@ def tile_picked_bilin_none_e_kernel(tc, xT, w1_words, w1_scales, fx, fy, offs, c
             for h in range(2):
                 nc.vector.tensor_copy(halves[h][:, :, j], planes[j][:].indirect(picks[:, 32 * h:32 * h + 32]))
         last = sb.tile([P, T], BF16, name="last")
-        for a, b in ((0, 1792), (3584, 3840), (3840, 4096)):
+        for a, b in ((0, 1792), (2944, 3200), (3584, 3840), (3840, 4096)):
             nc.scalar.copy(last[:, a:b], planes[3][:, a:b])
-        for a, b in ((1792, 3072), (3072, 3584)):
+        for a, b in ((1792, 2944), (3200, 3584)):
             nc.vector.tensor_copy(last[:, a:b], planes[3][:, a:b])
         nc.vector.tensor_copy(halves[0][:, :, 3], planes[3][:].indirect(picks[:, 0:32]))
         nc.scalar.activation(halves[1][:, :, 3], last[:].indirect(picks[:, 32:64]), COPY)

@@ -39,7 +39,7 @@ def tile_picked_bilin_none_e_kernel(tc, xT, w1_words, w1_scales, fx, fy, offs, c
         nc.sync.dma_start(picks[:], offs)
         for j in range(1, PACK - 1):
             nc.sync.dma_start(planes[j][:], rows[:, j, :])
-        pieces = ((0, 1792), (1792, 3200), (3200, 3840), (3840, 4096))
+        pieces = ((0, 1536), (1536, 3200), (3200, 3840), (3840, 4096))
         for a, b in pieces:
             nc.sync.dma_start(planes[3][:, a:b], rows[:, 3, a:b])
         wscale = sb.tile([P, N], U8, name="wscale", align_bytes=64)
@@ -80,9 +80,9 @@ def tile_picked_bilin_none_e_kernel(tc, xT, w1_words, w1_scales, fx, fy, offs, c
             for h in range(2):
                 nc.vector.tensor_copy(halves[h][:, :, j], planes[j][:].indirect(picks[:, 32 * h:32 * h + 32]))
         last = sb.tile([P, T], BF16, name="last")
-        for a, b in ((0, 1792), (2944, 3200), (3584, 3840), (3840, 4096)):
+        for a, b in ((0, 1536), (2560, 3200), (3584, 3840), (3840, 4096)):
             nc.scalar.copy(last[:, a:b], planes[3][:, a:b])
-        for a, b in ((1792, 2944), (3200, 3584)):
+        for a, b in ((1536, 2560), (3200, 3584)):
             nc.vector.tensor_copy(last[:, a:b], planes[3][:, a:b])
         nc.vector.tensor_copy(halves[0][:, :, 3], planes[3][:].indirect(picks[:, 0:32]))
         nc.scalar.activation(halves[1][:, :, 3], last[:].indirect(picks[:, 32:64]), COPY)

@@ -100,41 +100,53 @@ def tile_picked_bilin_none_e_kernel(tc, xT, w1_words, w1_scales, fx, fy, offs, c
             else:
                 nc.scalar.copy(dst, acc[:])
 
-        terms = [sb.tile([P, V], F32, name=f"term{i}") for i in range(3)]
-        sums = [ps.tile([P, P], F32, name=f"sum{k}", tag=f"bank{4 + k}") for k in range(4)]
+        shared = 3 * P
 
         def weigh(dst, i, a, b):
             nc.vector.tensor_tensor(dst, y[:].indirect(corners[i][:, a // 16:b // 16]), wts[i][:, a:b], MULT)
 
-        def add_up(i, k):
-            nc.tensor.matmul(sums[k][:], terms[i][:, k * P:(k + 1) * P], ident[:], start=(i == 0), stop=(i == 2), is_transpose=True)
+        raw = [sb.tile([P, shared], F32, name=f"raw{i}") for i in range(2)]
+        for a, b in ((0, 2 * P), (2 * P, shared)):
+            for i in range(2):
+                nc.scalar.activation(raw[i][:, a:b], y[:].indirect(corners[i][:, a // 16:b // 16]), COPY)
+        own = sb.tile([P, 3, P], F32, name="own")
+        for i in range(3):
+            weigh(own[:, i, :], i, shared, V)
+        third = sb.tile([P, shared], F32, name="third")
+        fourth = sb.tile([P, V], F32, name="fourth")
+        weigh(third[:], 2, 0, shared)
+        weigh(fourth[:, 0:shared], 3, 0, shared)
+        weigh(fourth[:, shared:V], 3, shared, V)
 
-        for i in range(2):
-            weigh(terms[i][:], i, 0, V)
-            for k in range(4):
-                add_up(i, k)
-        back01 = ps.tile([P, 2 * P], F32, name="back01", tag="bank0")
-        back2 = ps.tile([P, P], F32, name="back2", tag="bank1")
-        back3 = ps.tile([P, P], F32, name="back3", tag="bank2")
-        backs = (back01[:, 0:P], back01[:, P:2 * P], back2[:], back3[:])
-        for k0, k1 in ((0, 2), (2, 3), (3, 4)):
-            weigh(terms[2][:, k0 * P:k1 * P], 2, k0 * P, k1 * P)
-            for k in range(k0, k1):
-                add_up(2, k)
-                turned = sb.tile([P, P], F32, name=f"turned{k}", tag=f"turned{k}")
-                nc.scalar.copy(turned[:], sums[k][:])
-                nc.tensor.transpose(backs[k], turned[:], ident[:])
+        fwd = [ps.tile([P, 2, P], F32, name=f"fwd{k}", tag=f"bank{5 + k}") for k in range(3)]
+        fsum = ps.tile([P, P], F32, name="fsum", tag="bank0")
+        backs = [ps.tile([P, P], F32, name=f"back{k}", tag=f"bank{1 + k}") for k in range(4)]
+        turned = [sb.tile([P, 2, P], F32, name=f"turned{k}") for k in range(4)]
 
+        def forward(k):
+            for i in range(2):
+                nc.tensor.transpose(fwd[k][:, i, :], raw[i][:, k * P:(k + 1) * P], ident[:])
+
+        def scale_and_return(k):
+            for i in range(2):
+                nc.scalar.activation(turned[k][:, i, :], fwd[k][:, i, :], COPY, scale=wcol[:, i, k:k + 1])
+            for i in range(2):
+                nc.tensor.matmul(backs[k][:], turned[k][:, i, :], ident[:], start=(i == 0), stop=(i == 1), is_transpose=True)
+
+        for i in range(3):
+            nc.tensor.matmul(fsum[:], own[:, i, :], ident[:], start=(i == 0), stop=(i == 2), is_transpose=True)
+        for k in range(3):
+            forward(k)
+        scale_and_return(0)
+        scale_and_return(1)
+        nc.scalar.copy(turned[3][:, 0, :], fsum[:])
+        nc.tensor.transpose(backs[3][:], turned[3][:, 0, :], ident[:])
+        scale_and_return(2)
+
+        pair = sb.tile([P, shared], F32, name="pair")
+        nc.vector.tensor_tensor(pair[:], third[:], fourth[:, 0:shared], ADD)
         res = sb.tile([P, V], F32, name="res")
-        first = sb.tile([P, 448], F32, name="fourth_first")
-        weigh(first[:, 0:256], 3, 0, 256)
-        weigh(first[:, 256:448], 3, 256, 448)
-        nc.vector.tensor_tensor(res[:, 0:256], first[:, 0:256], back01[:], ADD)
-        nc.sync.dma_start(out[:, 0:256], res[:, 0:256])
-        rest = sb.tile([P, 64], F32, name="fourth_rest", tag="turned1")
-        weigh(rest[:], 3, 448, V)
-        nc.vector.tensor_tensor(res[:, 256:384], first[:, 256:384], back2[:], ADD)
-        nc.sync.dma_start(out[:, 256:384], res[:, 256:384])
-        nc.vector.tensor_tensor(res[:, 384:448], first[:, 384:448], back3[:, 0:64], ADD)
-        nc.vector.tensor_tensor(res[:, 448:V], rest[:], back3[:, 64:P], ADD)
-        nc.sync.dma_start(out[:, 384:V], res[:, 384:V])
+        for k in (0, 1, 3, 2):
+            mine = fourth[:, shared:V] if k == 3 else pair[:, k * P:(k + 1) * P]
+            nc.vector.tensor_tensor(res[:, k * P:(k + 1) * P], mine, backs[k][:], ADD)
+            nc.sync.dma_start(out[:, k * P:(k + 1) * P], res[:, k * P:(k + 1) * P])

@@ -69,10 +69,11 @@ def tile_picked_bilin_none_e_kernel(tc, xT, w1_words, w1_scales, fx, fy, offs, c
         wts = []
         for i in range(4):
             wps = ps.tile([P, V], F32, name=f"wps{i}", tag=f"bank{i + 3}")
-            for b in range(4):
+            first = 3 if i < 2 else 0
+            for b in range(first, 4):
                 nc.tensor.transpose(wps[:, b * P:(b + 1) * P], wcol[:, i, b:b + 1].to_broadcast([P, P]), ident[:])
             wt = sb.tile([P, V], F32, name=f"wt{i}")
-            nc.scalar.copy(wt[:], wps[:])
+            nc.scalar.copy(wt[:, first * P:V], wps[:, first * P:V])
             wts.append(wt)
 
         halves = [sb.tile([P, 512, PACK], BF16, name=f"xb{h}", align_bytes=64) for h in range(2)]

@@ -69,7 +69,7 @@ def tile_picked_bilin_none_e_kernel(tc, xT, w1_words, w1_scales, fx, fy, offs, c
         wts = []
         for i in range(4):
             wps = ps.tile([P, V], F32, name=f"wps{i}", tag=f"bank{i + 3}")
-            first = 3 if i < 2 else 0
+            first = 2 if i < 3 else 0
             for b in range(first, 4):
                 nc.tensor.transpose(wps[:, b * P:(b + 1) * P], wcol[:, i, b:b + 1].to_broadcast([P, P]), ident[:])
             wt = sb.tile([P, V], F32, name=f"wt{i}")
@@ -101,53 +101,44 @@ def tile_picked_bilin_none_e_kernel(tc, xT, w1_words, w1_scales, fx, fy, offs, c
             else:
                 nc.scalar.copy(dst, acc[:])
 
-        shared = 3 * P
+        shared = 2 * P
 
         def weigh(dst, i, a, b):
             nc.vector.tensor_tensor(dst, y[:].indirect(corners[i][:, a // 16:b // 16]), wts[i][:, a:b], MULT)
 
-        raw = [sb.tile([P, shared], F32, name=f"raw{i}") for i in range(2)]
-        for a, b in ((0, 2 * P), (2 * P, shared)):
-            for i in range(2):
-                nc.scalar.activation(raw[i][:, a:b], y[:].indirect(corners[i][:, a // 16:b // 16]), COPY)
-        own = sb.tile([P, 3, P], F32, name="own")
-        for i in range(3):
-            weigh(own[:, i, :], i, shared, V)
-        third = sb.tile([P, shared], F32, name="third")
-        fourth = sb.tile([P, V], F32, name="fourth")
-        weigh(third[:], 2, 0, shared)
-        weigh(fourth[:, 0:shared], 3, 0, shared)
-        weigh(fourth[:, shared:V], 3, shared, V)
+        raw = [sb.tile([P, shared], F32, name=f"raw{i}") for i in range(3)]
+        for i, a, b in ((0, 0, shared), (1, 0, shared), (2, 0, P), (2, P, shared)):
+            nc.scalar.activation(raw[i][:, a:b], y[:].indirect(corners[i][:, a // 16:b // 16]), COPY)
 
-        fwd = [ps.tile([P, 2, P], F32, name=f"fwd{k}", tag=f"bank{5 + k}") for k in range(3)]
-        fsum = ps.tile([P, P], F32, name="fsum", tag="bank0")
-        backs = [ps.tile([P, P], F32, name=f"back{k}", tag=f"bank{1 + k}") for k in range(4)]
-        turned = [sb.tile([P, 2, P], F32, name=f"turned{k}") for k in range(4)]
-
-        def forward(k):
-            for i in range(2):
-                nc.tensor.transpose(fwd[k][:, i, :], raw[i][:, k * P:(k + 1) * P], ident[:])
-
-        def scale_and_return(k):
-            for i in range(2):
-                nc.scalar.activation(turned[k][:, i, :], fwd[k][:, i, :], COPY, scale=wcol[:, i, k:k + 1])
-            for i in range(2):
-                nc.tensor.matmul(backs[k][:], turned[k][:, i, :], ident[:], start=(i == 0), stop=(i == 1), is_transpose=True)
-
-        for i in range(3):
-            nc.tensor.matmul(fsum[:], own[:, i, :], ident[:], start=(i == 0), stop=(i == 2), is_transpose=True)
-        for k in range(3):
-            forward(k)
-        scale_and_return(0)
-        scale_and_return(1)
-        nc.scalar.copy(turned[3][:, 0, :], fsum[:])
-        nc.tensor.transpose(backs[3][:], turned[3][:, 0, :], ident[:])
-        scale_and_return(2)
-
-        pair = sb.tile([P, shared], F32, name="pair")
-        nc.vector.tensor_tensor(pair[:], third[:], fourth[:, 0:shared], ADD)
+        own = [sb.tile([P, V - shared], F32, name=f"own{i}") for i in range(4)]
+        upper = sb.tile([P, V - shared], F32, name="upper")
+        three = sb.tile([P, V - shared], F32, name="three")
+        kept = sb.tile([P, shared], F32, name="kept")
         res = sb.tile([P, V], F32, name="res")
-        for k in (0, 1, 3, 2):
-            mine = fourth[:, shared:V] if k == 3 else pair[:, k * P:(k + 1) * P]
-            nc.vector.tensor_tensor(res[:, k * P:(k + 1) * P], mine, backs[k][:], ADD)
+        for i in range(3):
+            weigh(own[i][:], i, shared, V)
+        nc.vector.tensor_tensor(upper[:], own[0][:], own[1][:], ADD)
+        weigh(own[3][:], 3, shared, V)
+        nc.vector.tensor_tensor(three[:], upper[:], own[2][:], ADD)
+        weigh(kept[:], 3, 0, shared)
+        nc.vector.tensor_tensor(res[:, shared:V], three[:], own[3][:], ADD)
+        nc.sync.dma_start(out[:, shared:V], res[:, shared:V])
+
+        both = [ps.tile([P, 2, P], F32, name=f"both{i}", tag=f"bank{i}") for i in range(2)]
+        third = [ps.tile([P, P], F32, name=f"third{k}", tag=f"bank{3 + k}") for k in range(2)]
+        backs = [ps.tile([P, P], F32, name=f"back{k}", tag=f"bank{5 + k}") for k in range(2)]
+        turned = [sb.tile([P, 3, P], F32, name=f"turned{k}") for k in range(2)]
+
+        def fwd(i, k):
+            return both[i][:, k, :] if i < 2 else third[k][:]
+
+        for i in range(3):
+            for k in range(2):
+                nc.tensor.transpose(fwd(i, k), raw[i][:, k * P:(k + 1) * P], ident[:])
+        for k in range(2):
+            for i in range(3):
+                nc.scalar.activation(turned[k][:, i, :], fwd(i, k), COPY, scale=wcol[:, i, k:k + 1])
+                nc.tensor.matmul(backs[k][:], turned[k][:, i, :], ident[:], start=(i == 0), stop=(i == 2), is_transpose=True)
+        for k in range(2):
+            nc.vector.tensor_tensor(res[:, k * P:(k + 1) * P], kept[:, k * P:(k + 1) * P], backs[k][:], ADD)
             nc.sync.dma_start(out[:, k * P:(k + 1) * P], res[:, k * P:(k + 1) * P])

@@ -113,14 +113,15 @@ def tile_picked_bilin_none_e_kernel(tc, xT, w1_words, w1_scales, fx, fy, offs, c
         own = [sb.tile([P, V - shared], F32, name=f"own{i}") for i in range(4)]
         upper = sb.tile([P, V - shared], F32, name="upper")
         three = sb.tile([P, V - shared], F32, name="three")
-        kept = sb.tile([P, shared], F32, name="kept")
+        tail = 64
+        kept = sb.tile([P, shared - tail], F32, name="kept")
         res = sb.tile([P, V], F32, name="res")
         for i in range(3):
             weigh(own[i][:], i, shared, V)
         nc.vector.tensor_tensor(upper[:], own[0][:], own[1][:], ADD)
         weigh(own[3][:], 3, shared, V)
         nc.vector.tensor_tensor(three[:], upper[:], own[2][:], ADD)
-        weigh(kept[:], 3, 0, shared)
+        weigh(kept[:], 3, 0, shared - tail)
         nc.vector.tensor_tensor(res[:, shared:V], three[:], own[3][:], ADD)
         nc.sync.dma_start(out[:, shared:V], res[:, shared:V])
 
@@ -139,6 +140,9 @@ def tile_picked_bilin_none_e_kernel(tc, xT, w1_words, w1_scales, fx, fy, offs, c
             for i in range(3):
                 nc.scalar.activation(turned[k][:, i, :], fwd(i, k), COPY, scale=wcol[:, i, k:k + 1])
                 nc.tensor.matmul(backs[k][:], turned[k][:, i, :], ident[:], start=(i == 0), stop=(i == 2), is_transpose=True)
-        for k in range(2):
-            nc.vector.tensor_tensor(res[:, k * P:(k + 1) * P], kept[:, k * P:(k + 1) * P], backs[k][:], ADD)
-            nc.sync.dma_start(out[:, k * P:(k + 1) * P], res[:, k * P:(k + 1) * P])
+        weigh(turned[0][:, 1, 0:tail], 3, shared - tail, shared)
+        nc.vector.tensor_tensor(res[:, 0:P], kept[:, 0:P], backs[0][:], ADD)
+        nc.sync.dma_start(out[:, 0:P], res[:, 0:P])
+        nc.vector.tensor_tensor(res[:, P:shared - tail], kept[:, P:], backs[1][:, 0:P - tail], ADD)
+        nc.vector.tensor_tensor(res[:, shared - tail:shared], turned[0][:, 1, 0:tail], backs[1][:, P - tail:], ADD)
+        nc.sync.dma_start(out[:, P:shared], res[:, P:shared])

@@ -88,7 +88,7 @@ def tile_picked_bilin_none_e_kernel(tc, xT, w1_words, w1_scales, fx, fy, offs, c
         nc.vector.tensor_copy(halves[0][:, :, 3], planes[3][:].indirect(picks[:, 0:32]))
         nc.scalar.activation(halves[1][:, :, 3], last[:].indirect(picks[:, 32:64]), COPY)
         y = sb.tile([P, S], F32, name="y")
-        chunks = ((0, 0, 256), (0, 256, 256), (1, 0, 256), (1, 256, 128), (1, 384, 128))
+        chunks = ((0, 0, 256), (0, 256, 256), (1, 0, 128), (1, 128, 128), (1, 256, 128), (1, 384, 128))
         for ci, (h, c0, n) in enumerate(chunks):
             codes = sb.tile([P, n], U32, name=f"codes{ci}", align_bytes=64)
             scales = sb.tile([P, n], U8, name=f"scales{ci}", align_bytes=64)
@@ -96,7 +96,7 @@ def tile_picked_bilin_none_e_kernel(tc, xT, w1_words, w1_scales, fx, fy, offs, c
             acc = ps.tile([P, n], F32, name=f"acc{ci}", tag=f"bank{ci}")
             nc.tensor.matmul_mx(out=acc[:], lhsT=wwords[:].bitcast(FP4X4), lhsT_scale=wscale[:], rhs=codes[:].bitcast(FP8X4), rhs_scale=scales[:], start=True, stop=True)
             dst = y[:, 512 * h + c0:512 * h + c0 + n]
-            if ci in (2, ):
+            if ci == 4:
                 nc.vector.tensor_copy(dst, acc[:])
             else:
                 nc.scalar.copy(dst, acc[:])

@@ -88,18 +88,21 @@ def tile_picked_bilin_none_e_kernel(tc, xT, w1_words, w1_scales, fx, fy, offs, c
         nc.vector.tensor_copy(halves[0][:, :, 3], planes[3][:].indirect(picks[:, 0:32]))
         nc.scalar.activation(halves[1][:, :, 3], last[:].indirect(picks[:, 32:64]), COPY)
         y = sb.tile([P, S], F32, name="y")
-        chunks = ((0, 0, 256), (0, 256, 256), (1, 0, 128), (1, 128, 128), (1, 256, 128), (1, 384, 128))
-        for ci, (h, c0, n) in enumerate(chunks):
-            codes = sb.tile([P, n], U32, name=f"codes{ci}", align_bytes=64)
-            scales = sb.tile([P, n], U8, name=f"scales{ci}", align_bytes=64)
-            nc.vector.quantize_mx(out=codes[:].bitcast(FP8X4), scales=scales[:], in_=halves[h][:, c0:c0 + n, :].rearrange("p n j -> p (n j)"))
-            acc = ps.tile([P, n], F32, name=f"acc{ci}", tag=f"bank{ci}")
-            nc.tensor.matmul_mx(out=acc[:], lhsT=wwords[:].bitcast(FP4X4), lhsT_scale=wscale[:], rhs=codes[:].bitcast(FP8X4), rhs_scale=scales[:], start=True, stop=True)
-            dst = y[:, 512 * h + c0:512 * h + c0 + n]
-            if ci == 4:
-                nc.vector.tensor_copy(dst, acc[:])
+        banks = (256, 256, 128, 128, 128, 128)
+        start = 0
+        for bi, width in enumerate(banks):
+            acc = ps.tile([P, width], F32, name=f"acc{bi}", tag=f"bank{bi}")
+            for c0 in range(0, width, P):
+                h, cell = divmod(start + c0, 512)
+                codes = sb.tile([P, P], U32, name=f"codes{start + c0}", align_bytes=64)
+                scales = sb.tile([P, P], U8, name=f"scales{start + c0}", align_bytes=64)
+                nc.vector.quantize_mx(out=codes[:].bitcast(FP8X4), scales=scales[:], in_=halves[h][:, cell:cell + P, :].rearrange("p n j -> p (n j)"))
+                nc.tensor.matmul_mx(out=acc[:, c0:c0 + P], lhsT=wwords[:].bitcast(FP4X4), lhsT_scale=wscale[:], rhs=codes[:].bitcast(FP8X4), rhs_scale=scales[:], start=True, stop=True)
+            if bi == 4:
+                nc.vector.tensor_copy(y[:, start:start + width], acc[:])
             else:
-                nc.scalar.copy(dst, acc[:])
+                nc.scalar.copy(y[:, start:start + width], acc[:])
+            start += width
 
         shared = 2 * P
 

@@ -30,24 +30,23 @@ def tile_picked_bilin_none_e_kernel(tc, xT, w1_words, w1_scales, fx, fy, offs, c
         frows = sb.tile([P, P], F32, name="frows")
         nc.scalar.dma_start(frows[24:28, :], fx[0, :].rearrange("(b c) -> b c", b=4))
         nc.scalar.dma_start(frows[28:32, :], fy[0, :].rearrange("(b c) -> b c", b=4))
+        srows = sb.tile([4, 4, N], U8, name="srows")
+        nc.scalar.dma_start(srows[:].bitcast(I32), w1_scales[0].rearrange("(q r) c -> r q c", r=4).bitcast(I32))
         for lo, hi in ((0, 24), (32, 64), (64, 128)):
             nc.vector.memset(frows[lo:hi, :], 0.0)
         picks = sb.tile([P, S // 16], U16, name="picks")
         rows = xT.rearrange("(p j) t -> p j t", j=PACK)
-        planes = [sb.tile([P, T], F32, name=f"plane{j}") for j in range(PACK)]
+        planes = [sb.tile([P, T], F32, name=f"plane{j}", align_bytes=256) for j in range(PACK)]
         nc.sync.dma_start(planes[0][:], rows[:, 0, :])
         nc.sync.dma_start(picks[:], offs)
-        for j in range(1, PACK - 1):
+        for j in range(1, PACK):
             nc.sync.dma_start(planes[j][:], rows[:, j, :])
-        pieces = ((0, 1536), (1536, 3200), (3200, 3840), (3840, 4096))
-        for a, b in pieces:
-            nc.sync.dma_start(planes[3][:, a:b], rows[:, 3, a:b])
         wscale = sb.tile([P, N], U8, name="wscale", align_bytes=64)
         nc.gpsimd.memset(wscale[:], 0)
         wwords = sb.tile([P, 2 * N], U8, name="wwords", align_bytes=64)
         nc.sync.dma_start(wwords[:].bitcast(I32), w1_words[0].bitcast(I32))
         for q in range(4):
-            nc.sync.dma_start(wscale[32 * q:32 * q + 4, :].bitcast(I32), w1_scales[0, 4 * q:4 * q + 4, :].bitcast(I32))
+            nc.vector.tensor_copy(wscale[32 * q:32 * q + 4, :].bitcast(I32), srows[:, q, :].bitcast(I32))
         corners = []
         for i, src in enumerate((c00, c01, c10, c11)):
             lst = sb.tile([P, V // 16], U16, name=f"corner{i}")
@@ -76,33 +75,26 @@ def tile_picked_bilin_none_e_kernel(tc, xT, w1_words, w1_scales, fx, fy, offs, c
             nc.scalar.copy(wt[:, first * P:V], wps[:, first * P:V])
             wts.append(wt)
 
-        halves = [sb.tile([P, 512, PACK], BF16, name=f"xb{h}", align_bytes=64) for h in range(2)]
-        for j in range(PACK - 1):
-            for h in range(2):
-                nc.vector.tensor_copy(halves[h][:, :, j], planes[j][:].indirect(picks[:, 32 * h:32 * h + 32]))
-        last = sb.tile([P, T], BF16, name="last")
-        for a, b in ((0, 1536), (2560, 3200), (3584, 3840), (3840, 4096)):
-            nc.scalar.copy(last[:, a:b], planes[3][:, a:b])
-        for a, b in ((1536, 2560), (3200, 3584)):
-            nc.vector.tensor_copy(last[:, a:b], planes[3][:, a:b])
-        nc.vector.tensor_copy(halves[0][:, :, 3], planes[3][:].indirect(picks[:, 0:32]))
-        nc.scalar.activation(halves[1][:, :, 3], last[:].indirect(picks[:, 32:64]), COPY)
+        half = S // 2
+        halves = [sb.tile([P, half, PACK], BF16, name=f"xb{h}", align_bytes=64) for h in range(2)]
+        for j in range(PACK):
+            nc.vector.tensor_copy(halves[0][:, :, j], planes[j][:].indirect(picks[:, 0:half // 16]))
+            step = half if j < PACK - 1 else P
+            for a in range(0, half, step):
+                nc.scalar.activation(halves[1][:, a:a + step, j], planes[j][:].indirect(picks[:, (half + a) // 16:(half + a + step) // 16]), COPY)
         y = sb.tile([P, S], F32, name="y")
-        banks = (256, 256, 128, 128, 128, 128)
-        start = 0
-        for bi, width in enumerate(banks):
+        chunks = ((512, 256), (0, 256), (256, 256), (768, 128), (896, 128))
+        for bi, (start, width) in enumerate(chunks):
+            h, cell = divmod(start, half)
             acc = ps.tile([P, width], F32, name=f"acc{bi}", tag=f"bank{bi}")
-            for c0 in range(0, width, P):
-                h, cell = divmod(start + c0, 512)
-                codes = sb.tile([P, P], U32, name=f"codes{start + c0}", align_bytes=64)
-                scales = sb.tile([P, P], U8, name=f"scales{start + c0}", align_bytes=64)
-                nc.vector.quantize_mx(out=codes[:].bitcast(FP8X4), scales=scales[:], in_=halves[h][:, cell:cell + P, :].rearrange("p n j -> p (n j)"))
-                nc.tensor.matmul_mx(out=acc[:, c0:c0 + P], lhsT=wwords[:].bitcast(FP4X4), lhsT_scale=wscale[:], rhs=codes[:].bitcast(FP8X4), rhs_scale=scales[:], start=True, stop=True)
-            if bi == 4:
+            codes = sb.tile([P, width], U32, name=f"codes{bi}", align_bytes=64)
+            scales = sb.tile([P, width], U8, name=f"scales{bi}", align_bytes=64)
+            nc.vector.quantize_mx(out=codes[:].bitcast(FP8X4), scales=scales[:], in_=halves[h][:, cell:cell + width, :].rearrange("p n j -> p (n j)"))
+            nc.tensor.matmul_mx(out=acc[:], lhsT=wwords[:].bitcast(FP4X4), lhsT_scale=wscale[:], rhs=codes[:].bitcast(FP8X4), rhs_scale=scales[:], start=True, stop=True)
+            if bi == 3:
                 nc.vector.tensor_copy(y[:, start:start + width], acc[:])
             else:
                 nc.scalar.copy(y[:, start:start + width], acc[:])
-            start += width
 
         shared = 2 * P
 

@@ -75,26 +75,41 @@ def tile_picked_bilin_none_e_kernel(tc, xT, w1_words, w1_scales, fx, fy, offs, c
             nc.scalar.copy(wt[:, first * P:V], wps[:, first * P:V])
             wts.append(wt)
 
-        half = S // 2
-        halves = [sb.tile([P, half, PACK], BF16, name=f"xb{h}", align_bytes=64) for h in range(2)]
-        for j in range(PACK):
-            nc.vector.tensor_copy(halves[0][:, :, j], planes[j][:].indirect(picks[:, 0:half // 16]))
-            step = half if j < PACK - 1 else P
-            for a in range(0, half, step):
-                nc.scalar.activation(halves[1][:, a:a + step, j], planes[j][:].indirect(picks[:, (half + a) // 16:(half + a + step) // 16]), COPY)
+        xb = sb.tile([P, S, PACK], BF16, name="xb", align_bytes=64)
         y = sb.tile([P, S], F32, name="y")
-        chunks = ((512, 256), (0, 256), (256, 256), (768, 128), (896, 128))
-        for bi, (start, width) in enumerate(chunks):
-            h, cell = divmod(start, half)
-            acc = ps.tile([P, width], F32, name=f"acc{bi}", tag=f"bank{bi}")
-            codes = sb.tile([P, width], U32, name=f"codes{bi}", align_bytes=64)
-            scales = sb.tile([P, width], U8, name=f"scales{bi}", align_bytes=64)
-            nc.vector.quantize_mx(out=codes[:].bitcast(FP8X4), scales=scales[:], in_=halves[h][:, cell:cell + width, :].rearrange("p n j -> p (n j)"))
-            nc.tensor.matmul_mx(out=acc[:], lhsT=wwords[:].bitcast(FP4X4), lhsT_scale=wscale[:], rhs=codes[:].bitcast(FP8X4), rhs_scale=scales[:], start=True, stop=True)
-            if bi == 3:
-                nc.vector.tensor_copy(y[:, start:start + width], acc[:])
-            else:
-                nc.scalar.copy(y[:, start:start + width], acc[:])
+        of_vector = ((128, 256), (384, 608))
+        of_scalar = ((0, 128), (256, 384), (608, S))
+        last_of_scalar = ((0, 128), (256, 384), (608, 768), (768, 896), (896, S))
+        banks = (0, 0, 1, 1, 2, 2, 3, 4)
+        accs = [ps.tile([P, banks.count(b), P], F32, name=f"acc{b}", tag=f"bank{b}") for b in range(3)]
+
+        def project(blk):
+            bank = banks[blk]
+            if bank == len(accs):
+                accs.append(ps.tile([P, 1, P], F32, name=f"acc{bank}", tag=f"bank{bank}"))
+            first = banks.index(bank)
+            codes = sb.tile([P, P], U32, name=f"codes{blk}", align_bytes=64)
+            scales = sb.tile([P, P], U8, name=f"scales{blk}", align_bytes=64)
+            nc.vector.quantize_mx(out=codes[:].bitcast(FP8X4), scales=scales[:], in_=xb[:, blk * P:(blk + 1) * P, :].rearrange("p n j -> p (n j)"))
+            nc.tensor.matmul_mx(out=accs[bank][:, blk - first, :], lhsT=wwords[:].bitcast(FP4X4), lhsT_scale=wscale[:], rhs=codes[:].bitcast(FP8X4), rhs_scale=scales[:], start=True, stop=True)
+            if blk == len(banks) - 1:
+                nc.vector.tensor_copy(y[:, blk * P:S], accs[bank][:, 0, :])
+            elif banks[blk + 1] != bank:
+                nc.scalar.copy(y[:, first * P:(blk + 1) * P], accs[bank][:].rearrange("p s c -> p (s c)"))
+
+        for j in range(PACK):
+            last = j == PACK - 1
+            for a, b in last_of_scalar if last else of_scalar:
+                nc.scalar.activation(xb[:, a:b, j], planes[j][:].indirect(picks[:, a // 16:b // 16]), COPY)
+            dense = [sb.tile([P, b - a], BF16, name=f"dense{j}_{a}") for a, b in of_vector]
+            for piece, (a, b) in zip(dense, of_vector):
+                nc.vector.tensor_copy(piece[:], planes[j][:].indirect(picks[:, a // 16:b // 16]))
+            if last:
+                project(0)
+            for piece, (a, b) in zip(dense, of_vector):
+                nc.vector.tensor_copy(xb[:, a:b, j], piece[:])
+        for blk in range(1, len(banks)):
+            project(blk)
 
         shared = 2 * P
 

@@ -117,35 +117,54 @@ def tile_picked_bilin_none_e_kernel(tc, xT, w1_words, w1_scales, fx, fy, offs, c
             nc.vector.tensor_tensor(dst, y[:].indirect(corners[i][:, a // 16:b // 16]), wts[i][:, a:b], MULT)
 
         raw = [sb.tile([P, shared], F32, name=f"raw{i}") for i in range(3)]
-        for i, a, b in ((0, 0, shared), (1, 0, shared), (2, 0, P), (2, P, shared)):
-            nc.scalar.activation(raw[i][:, a:b], y[:].indirect(corners[i][:, a // 16:b // 16]), COPY)
-
         own = [sb.tile([P, V - shared], F32, name=f"own{i}") for i in range(4)]
-        upper = sb.tile([P, V - shared], F32, name="upper")
-        three = sb.tile([P, V - shared], F32, name="three")
-        tail = 64
-        kept = sb.tile([P, shared - tail], F32, name="kept")
-        res = sb.tile([P, V], F32, name="res")
-        for i in range(3):
-            weigh(own[i][:], i, shared, V)
-        nc.vector.tensor_tensor(upper[:], own[0][:], own[1][:], ADD)
-        weigh(own[3][:], 3, shared, V)
-        nc.vector.tensor_tensor(three[:], upper[:], own[2][:], ADD)
-        weigh(kept[:], 3, 0, shared - tail)
-        nc.vector.tensor_tensor(res[:, shared:V], three[:], own[3][:], ADD)
-        nc.sync.dma_start(out[:, shared:V], res[:, shared:V])
-
         both = [ps.tile([P, 2, P], F32, name=f"both{i}", tag=f"bank{i}") for i in range(2)]
         third = [ps.tile([P, P], F32, name=f"third{k}", tag=f"bank{3 + k}") for k in range(2)]
         backs = [ps.tile([P, P], F32, name=f"back{k}", tag=f"bank{5 + k}") for k in range(2)]
+        summed = ps.tile([P, P], F32, name="summed", tag="bank2")
+        home = ps.tile([P, P], F32, name="home", tag="bank7")
         turned = [sb.tile([P, 3, P], F32, name=f"turned{k}") for k in range(2)]
+        moved = sb.tile([P, P], F32, name="moved")
+        upper = sb.tile([P, P], F32, name="upper")
+        three = sb.tile([P, P], F32, name="three")
+        tail = 64
+        kept = sb.tile([P, shared - tail], F32, name="kept")
+        res = sb.tile([P, V], F32, name="res")
+
+        def fetch(i, a, b):
+            nc.scalar.activation(raw[i][:, a:b], y[:].indirect(corners[i][:, a // 16:b // 16]), COPY)
 
         def fwd(i, k):
             return both[i][:, k, :] if i < 2 else third[k][:]
 
-        for i in range(3):
+        def turn(i, k):
+            nc.tensor.transpose(fwd(i, k), raw[i][:, k * P:(k + 1) * P], ident[:])
+
+        fetch(0, 0, shared)
+        fetch(1, 0, shared)
+        fetch(2, 0, P)
+        fetch(2, P, shared)
+        for i in range(2):
+            weigh(own[i][:], i, shared, V)
+        weigh(own[2][:, 0:P], 2, shared, shared + P)
+        weigh(own[2][:, P:], 2, shared + P, V)
+        for i in range(2):
+            nc.tensor.matmul(summed[:], own[i][:, 0:P], ident[:], start=(i == 0), stop=False, is_transpose=True)
             for k in range(2):
-                nc.tensor.transpose(fwd(i, k), raw[i][:, k * P:(k + 1) * P], ident[:])
+                turn(i, k)
+        nc.tensor.matmul(summed[:], own[2][:, 0:P], ident[:], start=False, stop=True, is_transpose=True)
+        for k in range(2):
+            turn(2, k)
+        nc.scalar.copy(moved[:], summed[:])
+        nc.tensor.transpose(home[:], moved[:], ident[:])
+        nc.vector.tensor_tensor(upper[:], own[0][:, P:], own[1][:, P:], ADD)
+        weigh(own[3][:], 3, shared, V)
+        nc.vector.tensor_tensor(three[:], upper[:], own[2][:, P:], ADD)
+        weigh(kept[:], 3, 0, shared - tail)
+        nc.vector.tensor_tensor(res[:, shared + P:V], three[:], own[3][:, P:], ADD)
+        nc.vector.tensor_tensor(res[:, shared:shared + P], own[3][:, 0:P], home[:], ADD)
+        nc.sync.dma_start(out[:, shared:V], res[:, shared:V])
+
         for k in range(2):
             for i in range(3):
                 nc.scalar.activation(turned[k][:, i, :], fwd(i, k), COPY, scale=wcol[:, i, k:k + 1])

@@ -36,17 +36,14 @@ def tile_picked_bilin_none_e_kernel(tc, xT, w1_words, w1_scales, fx, fy, offs, c
             nc.vector.memset(frows[lo:hi, :], 0.0)
         picks = sb.tile([P, S // 16], U16, name="picks")
         rows = xT.rearrange("(p j) t -> p j t", j=PACK)
-        planes = [sb.tile([P, T], F32, name=f"plane{j}", align_bytes=256) for j in range(PACK)]
-        nc.sync.dma_start(planes[0][:], rows[:, 0, :])
+        front = sb.tile([P, 2, T], F32, name="front", align_bytes=256)
+        planes = {j: sb.tile([P, T], F32, name=f"plane{j}", align_bytes=256) for j in range(2, PACK)}
+        nc.sync.dma_start(front[:], rows[:, 0:2, :])
         nc.sync.dma_start(picks[:], offs)
-        for j in range(1, PACK):
+        for j in range(2, PACK):
             nc.sync.dma_start(planes[j][:], rows[:, j, :])
-        wscale = sb.tile([P, N], U8, name="wscale", align_bytes=64)
-        nc.gpsimd.memset(wscale[:], 0)
         wwords = sb.tile([P, 2 * N], U8, name="wwords", align_bytes=64)
         nc.sync.dma_start(wwords[:].bitcast(I32), w1_words[0].bitcast(I32))
-        for q in range(4):
-            nc.vector.tensor_copy(wscale[32 * q:32 * q + 4, :].bitcast(I32), srows[:, q, :].bitcast(I32))
         corners = []
         for i, src in enumerate((c00, c01, c10, c11)):
             lst = sb.tile([P, V // 16], U16, name=f"corner{i}")
@@ -97,7 +94,17 @@ def tile_picked_bilin_none_e_kernel(tc, xT, w1_words, w1_scales, fx, fy, offs, c
             elif banks[blk + 1] != bank:
                 nc.scalar.copy(y[:, first * P:(blk + 1) * P], accs[bank][:].rearrange("p s c -> p (s c)"))
 
-        for j in range(PACK):
+        split = 768
+        pair = sb.tile([P, 2, S - split], F32, name="pair", tag="pair", align_bytes=64)
+        for j in range(2):
+            nc.vector.tensor_copy(xb[:, 0:split, j], front[:, j, :].indirect(picks[:, 0:split // 16]))
+            nc.scalar.activation(pair[:, j, :], front[:, j, :].indirect(picks[:, split // 16:S // 16]), COPY)
+        nc.scalar.copy(xb[:, split:S, 0:2], pair[:].rearrange("p j n -> p n j"))
+        wscale = sb.tile([P, N], U8, name="wscale", tag="pair", align_bytes=64)
+        nc.vector.memset(wscale[:].bitcast(I32), 0)
+        for q in range(4):
+            nc.vector.tensor_copy(wscale[32 * q:32 * q + 4, :].bitcast(I32), srows[:, q, :].bitcast(I32))
+        for j in range(2, PACK):
             last = j == PACK - 1
             for a, b in last_of_scalar if last else of_scalar:
                 nc.scalar.activation(xb[:, a:b, j], planes[j][:].indirect(picks[:, a // 16:b // 16]), COPY)
@@ -162,8 +169,9 @@ def tile_picked_bilin_none_e_kernel(tc, xT, w1_words, w1_scales, fx, fy, offs, c
         nc.vector.tensor_tensor(three[:], upper[:], own[2][:, P:], ADD)
         weigh(kept[:], 3, 0, shared - tail)
         nc.vector.tensor_tensor(res[:, shared + P:V], three[:], own[3][:, P:], ADD)
+        nc.sync.dma_start(out[:, shared + P:V], res[:, shared + P:V])
         nc.vector.tensor_tensor(res[:, shared:shared + P], own[3][:, 0:P], home[:], ADD)
-        nc.sync.dma_start(out[:, shared:V], res[:, shared:V])
+        nc.sync.dma_start(out[:, shared:shared + P], res[:, shared:shared + P])
 
         for k in range(2):
             for i in range(3):

import concourse.mybir as mybir
from concourse.masks import make_identity
from contextlib import ExitStack

K, T, S, V, N = 512, 4096, 1024, 512, 128
FLOPS = 2 * K * S * N

F32 = mybir.dt.float32
BF16 = mybir.dt.bfloat16
I32 = mybir.dt.int32
U32 = mybir.dt.uint32
U16 = mybir.dt.uint16
U8 = mybir.dt.uint8
FP8X4 = mybir.dt.float8_e4m3fn_x4
FP4X4 = mybir.dt.float4_e2m1fn_x4
MULT = mybir.AluOpType.mult
ADD = mybir.AluOpType.add
COPY = mybir.ActivationFunctionType.Copy

P = 128
PACK = 4


def tile_picked_bilin_none_e_kernel(tc, xT, w1_words, w1_scales, fx, fy, offs, c00, c01, c10, c11, out):
    nc = tc.nc
    with ExitStack() as ctx:
        sb = ctx.enter_context(tc.tile_pool(name="sb", bufs=1))
        ps = ctx.enter_context(tc.psum_pool(name="ps", bufs=1))

        frows = sb.tile([P, P], F32, name="frows")
        nc.scalar.dma_start(frows[24:28, :], fx[0, :].rearrange("(b c) -> b c", b=4))
        nc.scalar.dma_start(frows[28:32, :], fy[0, :].rearrange("(b c) -> b c", b=4))
        srows = sb.tile([4, 4, N], U8, name="srows")
        nc.scalar.dma_start(srows[:].bitcast(I32), w1_scales[0].rearrange("(q r) c -> r q c", r=4).bitcast(I32))
        for lo, hi in ((0, 24), (32, 64), (64, 128)):
            nc.vector.memset(frows[lo:hi, :], 0.0)
        picks = sb.tile([P, S // 16], U16, name="picks")
        rows = xT.rearrange("(p j) t -> p j t", j=PACK)
        front = sb.tile([P, 2, T], F32, name="front", align_bytes=256)
        planes = {j: sb.tile([P, T], F32, name=f"plane{j}", align_bytes=256) for j in range(2, PACK)}
        nc.sync.dma_start(front[:], rows[:, 0:2, :])
        nc.sync.dma_start(picks[:], offs)
        for j in range(2, PACK):
            nc.sync.dma_start(planes[j][:], rows[:, j, :])
        wwords = sb.tile([P, 2 * N], U8, name="wwords", align_bytes=64)
        nc.sync.dma_start(wwords[:].bitcast(I32), w1_words[0].bitcast(I32))
        corners = []
        for i, src in enumerate((c00, c01, c10, c11)):
            lst = sb.tile([P, V // 16], U16, name=f"corner{i}")
            nc.sync.dma_start(lst[:], src)
            corners.append(lst)

        ident = sb.tile([P, P], F32, name="ident")
        make_identity(nc, ident[:])

        fps = ps.tile([P, P], F32, name="fps", tag="bank7")
        nc.tensor.transpose(fps[:], frows[:], ident[:])
        f = sb.tile([P, 2, 8], F32, name="f")
        nc.scalar.copy(f[:, 1, :], fps[:, 24:32])
        nc.scalar.activation(f[:, 0, :], fps[:, 24:32], COPY, bias=1.0, scale=-1.0)
        wcol = sb.tile([P, 4, 4], F32, name="wcol")
        for a in range(2):
            for b in range(2):
                nc.gpsimd.tensor_tensor(wcol[:, 2 * a + b, :], f[:, a, 4:8], f[:, b, 0:4], MULT)
        wts = []
        for i in range(4):
            wps = ps.tile([P, V], F32, name=f"wps{i}", tag=f"bank{i + 3}")
            first = 2 if i < 3 else 0
            for b in range(first, 4):
                nc.tensor.transpose(wps[:, b * P:(b + 1) * P], wcol[:, i, b:b + 1].to_broadcast([P, P]), ident[:])
            wt = sb.tile([P, V], F32, name=f"wt{i}")
            nc.scalar.copy(wt[:, first * P:V], wps[:, first * P:V])
            wts.append(wt)

        xb = sb.tile([P, S, PACK], BF16, name="xb", align_bytes=64)
        y = sb.tile([P, S], F32, name="y")
        of_vector = ((128, 256), (384, 608))
        of_scalar = ((0, 128), (256, 384), (608, S))
        last_of_scalar = ((0, 128), (256, 384), (608, 768), (768, 896), (896, S))
        banks = (0, 0, 1, 1, 2, 2, 3, 4)
        accs = [ps.tile([P, banks.count(b), P], F32, name=f"acc{b}", tag=f"bank{b}") for b in range(3)]

        def project(blk):
            bank = banks[blk]
            if bank == len(accs):
                accs.append(ps.tile([P, 1, P], F32, name=f"acc{bank}", tag=f"bank{bank}"))
            first = banks.index(bank)
            codes = sb.tile([P, P], U32, name=f"codes{blk}", align_bytes=64)
            scales = sb.tile([P, P], U8, name=f"scales{blk}", align_bytes=64)
            nc.vector.quantize_mx(out=codes[:].bitcast(FP8X4), scales=scales[:], in_=xb[:, blk * P:(blk + 1) * P, :].rearrange("p n j -> p (n j)"))
            nc.tensor.matmul_mx(out=accs[bank][:, blk - first, :], lhsT=wwords[:].bitcast(FP4X4), lhsT_scale=wscale[:], rhs=codes[:].bitcast(FP8X4), rhs_scale=scales[:], start=True, stop=True)
            if blk == len(banks) - 1:
                nc.vector.tensor_copy(y[:, blk * P:S], accs[bank][:, 0, :])
            elif banks[blk + 1] != bank:
                nc.scalar.copy(y[:, first * P:(blk + 1) * P], accs[bank][:].rearrange("p s c -> p (s c)"))

        split = 768
        pair = sb.tile([P, 2, S - split], F32, name="pair", tag="pair", align_bytes=64)
        for j in range(2):
            nc.vector.tensor_copy(xb[:, 0:split, j], front[:, j, :].indirect(picks[:, 0:split // 16]))
            nc.scalar.activation(pair[:, j, :], front[:, j, :].indirect(picks[:, split // 16:S // 16]), COPY)
        nc.scalar.copy(xb[:, split:S, 0:2], pair[:].rearrange("p j n -> p n j"))
        wscale = sb.tile([P, N], U8, name="wscale", tag="pair", align_bytes=64)
        nc.vector.memset(wscale[:].bitcast(I32), 0)
        for q in range(4):
            nc.vector.tensor_copy(wscale[32 * q:32 * q + 4, :].bitcast(I32), srows[:, q, :].bitcast(I32))
        for j in range(2, PACK):
            last = j == PACK - 1
            for a, b in last_of_scalar if last else of_scalar:
                nc.scalar.activation(xb[:, a:b, j], planes[j][:].indirect(picks[:, a // 16:b // 16]), COPY)
            dense = [sb.tile([P, b - a], BF16, name=f"dense{j}_{a}") for a, b in of_vector]
            for piece, (a, b) in zip(dense, of_vector):
                nc.vector.tensor_copy(piece[:], planes[j][:].indirect(picks[:, a // 16:b // 16]))
            if last:
                project(0)
            for piece, (a, b) in zip(dense, of_vector):
                nc.vector.tensor_copy(xb[:, a:b, j], piece[:])
        for blk in range(1, len(banks)):
            project(blk)

        shared = 2 * P

        def weigh(dst, i, a, b):
            nc.vector.tensor_tensor(dst, y[:].indirect(corners[i][:, a // 16:b // 16]), wts[i][:, a:b], MULT)

        raw = [sb.tile([P, shared], F32, name=f"raw{i}") for i in range(3)]
        own = [sb.tile([P, V - shared], F32, name=f"own{i}") for i in range(4)]
        both = [ps.tile([P, 2, P], F32, name=f"both{i}", tag=f"bank{i}") for i in range(2)]
        third = [ps.tile([P, P], F32, name=f"third{k}", tag=f"bank{3 + k}") for k in range(2)]
        backs = [ps.tile([P, P], F32, name=f"back{k}", tag=f"bank{5 + k}") for k in range(2)]
        summed = ps.tile([P, P], F32, name="summed", tag="bank2")
        home = ps.tile([P, P], F32, name="home", tag="bank7")
        turned = [sb.tile([P, 3, P], F32, name=f"turned{k}") for k in range(2)]
        moved = sb.tile([P, P], F32, name="moved")
        upper = sb.tile([P, P], F32, name="upper")
        three = sb.tile([P, P], F32, name="three")
        tail = 64
        kept = sb.tile([P, shared - tail], F32, name="kept")
        res = sb.tile([P, V], F32, name="res")

        def fetch(i, a, b):
            nc.scalar.activation(raw[i][:, a:b], y[:].indirect(corners[i][:, a // 16:b // 16]), COPY)

        def fwd(i, k):
            return both[i][:, k, :] if i < 2 else third[k][:]

        def turn(i, k):
            nc.tensor.transpose(fwd(i, k), raw[i][:, k * P:(k + 1) * P], ident[:])

        fetch(0, 0, shared)
        fetch(1, 0, shared)
        fetch(2, 0, P)
        fetch(2, P, shared)
        for i in range(2):
            weigh(own[i][:], i, shared, V)
        weigh(own[2][:, 0:P], 2, shared, shared + P)
        weigh(own[2][:, P:], 2, shared + P, V)
        for i in range(2):
            nc.tensor.matmul(summed[:], own[i][:, 0:P], ident[:], start=(i == 0), stop=False, is_transpose=True)
            for k in range(2):
                turn(i, k)
        nc.tensor.matmul(summed[:], own[2][:, 0:P], ident[:], start=False, stop=True, is_transpose=True)
        for k in range(2):
            turn(2, k)
        nc.scalar.copy(moved[:], summed[:])
        nc.tensor.transpose(home[:], moved[:], ident[:])
        nc.vector.tensor_tensor(upper[:], own[0][:, P:], own[1][:, P:], ADD)
        weigh(own[3][:], 3, shared, V)
        nc.vector.tensor_tensor(three[:], upper[:], own[2][:, P:], ADD)
        weigh(kept[:], 3, 0, shared - tail)
        nc.vector.tensor_tensor(res[:, shared + P:V], three[:], own[3][:, P:], ADD)
        nc.sync.dma_start(out[:, shared + P:V], res[:, shared + P:V])
        nc.vector.tensor_tensor(res[:, shared:shared + P], own[3][:, 0:P], home[:], ADD)
        nc.sync.dma_start(out[:, shared:shared + P], res[:, shared:shared + P])

        for k in range(2):
            for i in range(3):
                nc.scalar.activation(turned[k][:, i, :], fwd(i, k), COPY, scale=wcol[:, i, k:k + 1])
                nc.tensor.matmul(backs[k][:], turned[k][:, i, :], ident[:], start=(i == 0), stop=(i == 2), is_transpose=True)
        weigh(turned[0][:, 1, 0:tail], 3, shared - tail, shared)
        nc.vector.tensor_tensor(res[:, 0:P], kept[:, 0:P], backs[0][:], ADD)
        nc.sync.dma_start(out[:, 0:P], res[:, 0:P])
        nc.vector.tensor_tensor(res[:, P:shared - tail], kept[:, P:], backs[1][:, 0:P - tail], ADD)
        nc.vector.tensor_tensor(res[:, shared - tail:shared], turned[0][:, 1, 0:tail], backs[1][:, P - tail:], ADD)
        nc.sync.dma_start(out[:, P:shared], res[:, P:shared])
